import numpy as np
import ml_dtypes


def mxq(x, axis, fmt="e4m3"):
    dtype, down = {"e4m3": (ml_dtypes.float8_e4m3fn, 7), "e5m2": (ml_dtypes.float8_e5m2, 14)}[fmt]
    v = np.moveaxis(np.asarray(x, np.float32).astype(ml_dtypes.bfloat16).astype(np.float64), axis, -1)
    blocks = v.reshape(v.shape[:-1] + (-1, 32))
    amax = np.abs(blocks).max(-1, keepdims=True)
    byte = np.maximum(np.where(amax > 0, np.frexp(amax)[1] - 1 + 127, 0) - down, 1)
    scale = np.exp2(byte - 127.0)
    codes = (blocks / scale).astype(np.float32).astype(dtype).astype(np.float64)
    return np.moveaxis((codes * scale).reshape(v.shape), -1, axis)


WIDE = False


def mx_kscale(k):
    if not WIDE:
        return np.ones(k)
    levels = np.array([10, -10, 5, -5, 0])
    if k % 512:
        return np.exp2(np.random.permutation(np.resize(levels, k // 32))).repeat(32)
    a = np.empty((k // 512, 16))
    for p in range(k // 512):
        a[p, :8] = np.random.permutation(np.resize(levels, 8))
        for g in range(8):
            far = levels[np.abs(levels - a[p, g]) >= 10]
            a[p, g + 8] = far[np.random.randint(len(far))]
    return np.exp2(a.ravel()).repeat(32)


def f64(x):
    return np.asarray(x).astype(np.float64)


def striped(idx):
    return np.tile(np.asarray(idx).reshape(-1, 16).T, (8, 1)).astype(np.uint16)


def unstriped(offs):
    return offs[:16].T.reshape(-1).astype(np.int64)


E2M1 = np.array([0.0, 0.5, 1.0, 1.5, 2.0, 3.0, 4.0, 6.0, -0.0, -0.5, -1.0, -1.5, -2.0, -3.0, -4.0, -6.0])


def pack_weight(w, fmt):
    k, n = w.shape
    w = f64(np.asarray(w, np.float32).astype(ml_dtypes.bfloat16)).reshape(k // 32, 32, n)
    amax = np.abs(w).max(1)
    if fmt == "e4m3":
        byte = np.frexp(amax)[1] - 1 + 127 - 7
    else:
        mant, ex = np.frexp(amax / 6.0)
        byte = np.where(mant > 0.5, ex, ex - 1) + 127
    byte = np.clip(np.where(amax > 0, byte, 1), 1, 254)
    scaled = (w * np.exp2(127.0 - byte)[:, None, :]).reshape(k, n).astype(np.float32)
    by_word = np.ascontiguousarray(scaled.reshape(k // 512, 128, 4, n).transpose(0, 1, 3, 2))
    if fmt == "e4m3":
        words = by_word.astype(ml_dtypes.float8_e4m3fn).view(np.uint8)
    else:
        c = by_word.astype(ml_dtypes.float4_e2m1fn).view(np.uint8) & 0xF
        words = (c[..., 0::2] | (c[..., 1::2] << 4)).reshape(k // 512, 128, 2 * n)
    return np.ascontiguousarray(words), np.ascontiguousarray(byte.astype(np.uint8).reshape(k // 512, 16, n))


def unpack_weight(words, scales, fmt):
    g, _, n = scales.shape
    words = np.ascontiguousarray(words).reshape(g, 128, n, -1)
    if fmt == "e4m3":
        vals = words.view(ml_dtypes.float8_e4m3fn).astype(np.float64)
    else:
        nib = np.empty((g, 128, n, 4), np.uint8)
        nib[..., 0::2] = words & 0xF
        nib[..., 1::2] = words >> 4
        vals = E2M1[nib]
    vals = vals * np.repeat(np.exp2(scales.astype(np.float64) - 127.0), 8, axis=1)[..., None]
    return vals.transpose(0, 1, 3, 2).reshape(g * 512, n)


B, N, T, D, DV, NQ = 1, 512, 1024, 512, 0, 128


def setup_inputs():
    n = np.random.standard_normal
    idx = np.random.permutation(T)[:B * N]
    s = mx_kscale(D)[:, None]
    kp = pack_weight(n((D, T)) / s, "e4m3")
    return {
        "qT": (n((B, D, NQ)) * s * (1.00 / np.sqrt(D))).astype(np.float32),
        "k_words": kp[0],
        "k_scales": kp[1],
        "offs": striped(idx),
    }


def reference(qT, k_words, k_scales, offs):
    idx = unstriped(offs)
    pool = unpack_weight(k_words, k_scales, "e4m3")
    pick = lambda x: x[:, idx].reshape(x.shape[0], B, N).transpose(1, 0, 2)
    a = mxq(f64(qT), 1, "e4m3").transpose(0, 2, 1) @ pick(pool)
    out = np.zeros((B, NQ, T))
    for b in range(B):
        out[b][:, idx[b * N:(b + 1) * N]] = a[b]
    return out

@@ -1,0 +1,88 @@
+from contextlib import ExitStack
+
+import concourse.mybir as mybir
+
+F32 = mybir.dt.float32
+BF16 = mybir.dt.bfloat16
+I32 = mybir.dt.int32
+U32 = mybir.dt.uint32
+U16 = mybir.dt.uint16
+U8 = mybir.dt.uint8
+FP8X4 = mybir.dt.float8_e4m3fn_x4
+
+P = 128
+PACK = 4
+SLOTS = 512
+TOKENS = 1024
+QUERIES = 128
+FEATURES = 512
+LIST_ROWS = 16
+FLOPS = 2 * FEATURES * QUERIES * SLOTS
+
+WORD_GATHERS = [(0, 128), (128, 256), (256, 512)]
+MATMULS = [(0, 128), (128, 256), (256, 384), (384, 512)]
+SCATTERS = [(0, 128), (128, 512)]
+
+
+def tile_attend_sddmm_kernel(tc, qT, k_words, k_scales, offs, out):
+    nc = tc.nc
+    with ExitStack() as ctx:
+        keep = ctx.enter_context(tc.tile_pool(name="keep", bufs=1))
+        psum = ctx.enter_context(tc.psum_pool(name="psum", bufs=1))
+
+        offsets = keep.tile([P, SLOTS // LIST_ROWS], U16, name="offsets")
+        pool_words = keep.tile([P, TOKENS], I32, name="pool_words", align_bytes=64)
+        pool_scales = keep.tile([P, TOKENS], U8, name="pool_scales", align_bytes=64)
+        q_raw = keep.tile([P, PACK, QUERIES], F32, name="q_raw", align_bytes=64)
+        q_grouped = keep.tile([P, QUERIES, PACK], BF16, name="q_grouped", align_bytes=64)
+        q_codes = keep.tile([P, QUERIES], U32, name="q_codes", align_bytes=64)
+        q_scales = keep.tile([P, QUERIES], U8, name="q_scales", align_bytes=64)
+        key_words = keep.tile([P, SLOTS], U32, name="key_words", align_bytes=64)
+        key_scales = keep.tile([P, SLOTS], U8, name="key_scales", align_bytes=64)
+        scores = keep.tile([P, SLOTS], F32, name="scores", align_bytes=64)
+        placed = keep.tile([P, TOKENS], F32, name="placed", align_bytes=64)
+
+        def listed(lo, hi):
+            return offsets[:, lo // LIST_ROWS : hi // LIST_ROWS]
+
+        nc.sync.dma_start(offsets[:], offs)
+        nc.vector.memset(pool_scales[:].bitcast(I32), 0)
+        for quad in range(4):
+            queue = nc.sync if quad % 2 == 0 else nc.scalar
+            queue.dma_start(
+                pool_scales[32 * quad : 32 * quad + 4, :].bitcast(I32),
+                k_scales[0, 4 * quad : 4 * quad + 4, :].bitcast(I32),
+            )
+        nc.sync.dma_start(q_raw[:], qT[0].rearrange("(p j) w -> p j w", j=PACK))
+        nc.sync.dma_start(pool_words[:], k_words[0].rearrange("p n t -> p (n t)").bitcast(I32))
+        nc.vector.memset(placed[:], 0.0)
+
+        nc.vector.tensor_copy(key_scales[:], pool_scales[:].indirect(offsets[:]))
+
+        nc.scalar.copy(out=q_grouped[:], in_=q_raw[:].rearrange("p j w -> p w j"))
+        nc.vector.quantize_mx(
+            out=q_codes[:].bitcast(FP8X4),
+            scales=q_scales[:],
+            in_=q_grouped[:].rearrange("p w j -> p (w j)"),
+        )
+
+        for lo, hi in WORD_GATHERS:
+            nc.vector.tensor_copy(key_words[:, lo:hi], pool_words[:].bitcast(U32).indirect(listed(lo, hi)))
+
+        for lo, hi in MATMULS:
+            acc = psum.tile([P, hi - lo], F32, name="acc%d" % lo)
+            nc.tensor.matmul_mx(
+                out=acc[:],
+                lhsT=q_codes[:].bitcast(FP8X4),
+                lhsT_scale=q_scales[:],
+                rhs=key_words[:, lo:hi].bitcast(FP8X4),
+                rhs_scale=key_scales[:, lo:hi],
+                start=True,
+                stop=True,
+            )
+            nc.scalar.copy(out=scores[:, lo:hi], in_=acc[:])
+
+        for lo, hi in SCATTERS:
+            nc.vector.tensor_copy(placed[:].indirect(listed(lo, hi)), scores[:, lo:hi])
+
+        nc.sync.dma_start(out[0], placed[:])

@@ -46,16 +46,16 @@ def tile_attend_sddmm_kernel(tc, qT, k_words, k_scales, offs, out):
             return offsets[:, lo // LIST_ROWS : hi // LIST_ROWS]
 
         nc.sync.dma_start(offsets[:], offs)
+        nc.scalar.dma_start(q_raw[:], qT[0].rearrange("(p j) w -> p j w", j=PACK))
         nc.vector.memset(pool_scales[:].bitcast(I32), 0)
-        for quad in range(4):
-            queue = nc.sync if quad % 2 == 0 else nc.scalar
-            queue.dma_start(
-                pool_scales[32 * quad : 32 * quad + 4, :].bitcast(I32),
-                k_scales[0, 4 * quad : 4 * quad + 4, :].bitcast(I32),
-            )
-        nc.sync.dma_start(q_raw[:], qT[0].rearrange("(p j) w -> p j w", j=PACK))
+        nc.sync.dma_start(pool_scales[0:4, :].bitcast(I32), k_scales[0, 0:4, :].bitcast(I32))
+        nc.scalar.dma_start(pool_scales[32:36, :].bitcast(I32), k_scales[0, 4:8, :].bitcast(I32))
+        nc.sync.dma_start(pool_scales[64:68, :].bitcast(I32), k_scales[0, 8:12, :].bitcast(I32))
+        nc.scalar.dma_start(pool_scales[96:100, :].bitcast(I32), k_scales[0, 12:16, :].bitcast(I32))
         nc.sync.dma_start(pool_words[:], k_words[0].rearrange("p n t -> p (n t)").bitcast(I32))
         nc.vector.memset(placed[:], 0.0)
+        warm = keep.tile([P, 1], F32, name="warm")
+        nc.scalar.copy(out=warm[:], in_=placed[:, 0:1])
 
         nc.vector.tensor_copy(key_scales[:], pool_scales[:].indirect(offsets[:]))
 

@@ -51,11 +51,9 @@ def tile_attend_sddmm_kernel(tc, qT, k_words, k_scales, offs, out):
         nc.sync.dma_start(pool_scales[0:4, :].bitcast(I32), k_scales[0, 0:4, :].bitcast(I32))
         nc.scalar.dma_start(pool_scales[32:36, :].bitcast(I32), k_scales[0, 4:8, :].bitcast(I32))
         nc.sync.dma_start(pool_scales[64:68, :].bitcast(I32), k_scales[0, 8:12, :].bitcast(I32))
-        nc.scalar.dma_start(pool_scales[96:100, :].bitcast(I32), k_scales[0, 12:16, :].bitcast(I32))
+        nc.sync.dma_start(pool_scales[96:100, :].bitcast(I32), k_scales[0, 12:16, :].bitcast(I32))
         nc.sync.dma_start(pool_words[:], k_words[0].rearrange("p n t -> p (n t)").bitcast(I32))
         nc.vector.memset(placed[:], 0.0)
-        warm = keep.tile([P, 1], F32, name="warm")
-        nc.scalar.copy(out=warm[:], in_=placed[:, 0:1])
 
         nc.vector.tensor_copy(key_scales[:], pool_scales[:].indirect(offsets[:]))
 

@@ -48,10 +48,8 @@ def tile_attend_sddmm_kernel(tc, qT, k_words, k_scales, offs, out):
         nc.sync.dma_start(offsets[:], offs)
         nc.scalar.dma_start(q_raw[:], qT[0].rearrange("(p j) w -> p j w", j=PACK))
         nc.vector.memset(pool_scales[:].bitcast(I32), 0)
-        nc.sync.dma_start(pool_scales[0:4, :].bitcast(I32), k_scales[0, 0:4, :].bitcast(I32))
-        nc.scalar.dma_start(pool_scales[32:36, :].bitcast(I32), k_scales[0, 4:8, :].bitcast(I32))
-        nc.sync.dma_start(pool_scales[64:68, :].bitcast(I32), k_scales[0, 8:12, :].bitcast(I32))
-        nc.sync.dma_start(pool_scales[96:100, :].bitcast(I32), k_scales[0, 12:16, :].bitcast(I32))
+        for row, queue in enumerate((nc.sync, nc.scalar, nc.sync, nc.sync)):
+            queue.dma_start(pool_scales[row:P:32, :].bitcast(I32), k_scales[0, row:16:4, :].bitcast(I32))
         nc.sync.dma_start(pool_words[:], k_words[0].rearrange("p n t -> p (n t)").bitcast(I32))
         nc.vector.memset(placed[:], 0.0)
 

@@ -81,4 +81,4 @@ def tile_attend_sddmm_kernel(tc, qT, k_words, k_scales, offs, out):
         for lo, hi in SCATTERS:
             nc.vector.tensor_copy(placed[:].indirect(listed(lo, hi)), scores[:, lo:hi])
 
-        nc.sync.dma_start(out[0], placed[:])
+        nc.scalar.dma_start(out[0], placed[:])

@@ -45,8 +45,8 @@ def tile_attend_sddmm_kernel(tc, qT, k_words, k_scales, offs, out):
         def listed(lo, hi):
             return offsets[:, lo // LIST_ROWS : hi // LIST_ROWS]
 
+        nc.sync.dma_start(q_raw[:], qT[0].rearrange("(p j) w -> p j w", j=PACK))
         nc.sync.dma_start(offsets[:], offs)
-        nc.scalar.dma_start(q_raw[:], qT[0].rearrange("(p j) w -> p j w", j=PACK))
         nc.vector.memset(pool_scales[:].bitcast(I32), 0)
         for row, queue in enumerate((nc.sync, nc.scalar, nc.sync, nc.sync)):
             queue.dma_start(pool_scales[row:P:32, :].bitcast(I32), k_scales[0, row:16:4, :].bitcast(I32))

@@ -21,6 +21,7 @@ FLOPS = 2 * FEATURES * QUERIES * SLOTS
 
 WORD_GATHERS = [(0, 128), (128, 256), (256, 512)]
 MATMULS = [(0, 128), (128, 256), (256, 384), (384, 512)]
+EARLY_SCALES = 384
 SCATTERS = [(0, 128), (128, 512)]
 
 
@@ -38,7 +39,7 @@ def tile_attend_sddmm_kernel(tc, qT, k_words, k_scales, offs, out):
         q_codes = keep.tile([P, QUERIES], U32, name="q_codes", align_bytes=64)
         q_scales = keep.tile([P, QUERIES], U8, name="q_scales", align_bytes=64)
         key_words = keep.tile([P, SLOTS], U32, name="key_words", align_bytes=64)
-        key_scales = keep.tile([P, SLOTS], U8, name="key_scales", align_bytes=64)
+        key_scales = keep.tile([P, EARLY_SCALES], U8, name="key_scales", align_bytes=64)
         scores = keep.tile([P, SLOTS], F32, name="scores", align_bytes=64)
         placed = keep.tile([P, TOKENS], F32, name="placed", align_bytes=64)
 
@@ -53,9 +54,12 @@ def tile_attend_sddmm_kernel(tc, qT, k_words, k_scales, offs, out):
         nc.sync.dma_start(pool_words[:], k_words[0].rearrange("p n t -> p (n t)").bitcast(I32))
         nc.vector.memset(placed[:], 0.0)
 
-        nc.vector.tensor_copy(key_scales[:], pool_scales[:].indirect(offsets[:]))
+        nc.vector.tensor_copy(key_scales[:], pool_scales[:].indirect(listed(0, EARLY_SCALES)))
 
-        nc.scalar.copy(out=q_grouped[:], in_=q_raw[:].rearrange("p j w -> p w j"))
+        nc.scalar.copy(
+            out=q_grouped[:].rearrange("p (c i) j -> p c j i", i=4),
+            in_=q_raw[:].rearrange("p j (c i) -> p c j i", i=4),
+        )
         nc.vector.quantize_mx(
             out=q_codes[:].bitcast(FP8X4),
             scales=q_scales[:],
@@ -66,13 +70,15 @@ def tile_attend_sddmm_kernel(tc, qT, k_words, k_scales, offs, out):
             nc.vector.tensor_copy(key_words[:, lo:hi], pool_words[:].bitcast(U32).indirect(listed(lo, hi)))
 
         for lo, hi in MATMULS:
+            if lo == EARLY_SCALES:
+                nc.vector.tensor_copy(key_scales[:, : hi - lo], pool_scales[:].indirect(listed(lo, hi)))
             acc = psum.tile([P, hi - lo], F32, name="acc%d" % lo)
             nc.tensor.matmul_mx(
                 out=acc[:],
                 lhsT=q_codes[:].bitcast(FP8X4),
                 lhsT_scale=q_scales[:],
                 rhs=key_words[:, lo:hi].bitcast(FP8X4),
-                rhs_scale=key_scales[:, lo:hi],
+                rhs_scale=key_scales[:, lo % EARLY_SCALES : lo % EARLY_SCALES + hi - lo],
                 start=True,
                 stop=True,
             )

@@ -87,4 +87,6 @@ def tile_attend_sddmm_kernel(tc, qT, k_words, k_scales, offs, out):
         for lo, hi in SCATTERS:
             nc.vector.tensor_copy(placed[:].indirect(listed(lo, hi)), scores[:, lo:hi])
 
-        nc.scalar.dma_start(out[0], placed[:])
+        half = TOKENS // 2
+        nc.sync.dma_start(out[0, :, :half], placed[:, :half])
+        nc.scalar.dma_start(out[0, :, half:], placed[:, half:])

@@ -46,8 +46,8 @@ def tile_attend_sddmm_kernel(tc, qT, k_words, k_scales, offs, out):
         def listed(lo, hi):
             return offsets[:, lo // LIST_ROWS : hi // LIST_ROWS]
 
-        nc.sync.dma_start(q_raw[:], qT[0].rearrange("(p j) w -> p j w", j=PACK))
         nc.sync.dma_start(offsets[:], offs)
+        nc.sync.dma_start(q_raw[:], qT[0].rearrange("(p j) w -> p j w", j=PACK))
         nc.vector.memset(pool_scales[:].bitcast(I32), 0)
         for row, queue in enumerate((nc.sync, nc.scalar, nc.sync, nc.sync)):
             queue.dma_start(pool_scales[row:P:32, :].bitcast(I32), k_scales[0, row:16:4, :].bitcast(I32))
@@ -56,15 +56,17 @@ def tile_attend_sddmm_kernel(tc, qT, k_words, k_scales, offs, out):
 
         nc.vector.tensor_copy(key_scales[:], pool_scales[:].indirect(listed(0, EARLY_SCALES)))
 
-        nc.scalar.copy(
-            out=q_grouped[:].rearrange("p (c i) j -> p c j i", i=4),
-            in_=q_raw[:].rearrange("p j (c i) -> p c j i", i=4),
-        )
-        nc.vector.quantize_mx(
-            out=q_codes[:].bitcast(FP8X4),
-            scales=q_scales[:],
-            in_=q_grouped[:].rearrange("p w j -> p (w j)"),
-        )
+        for lo in range(0, QUERIES, QUERIES // 2):
+            hi = lo + QUERIES // 2
+            nc.scalar.copy(
+                out=q_grouped[:, lo:hi, :].rearrange("p (c i) j -> p c j i", i=4),
+                in_=q_raw[:, :, lo:hi].rearrange("p j (c i) -> p c j i", i=4),
+            )
+            nc.vector.quantize_mx(
+                out=q_codes[:, lo:hi].bitcast(FP8X4),
+                scales=q_scales[:, lo:hi],
+                in_=q_grouped[:, lo:hi, :].rearrange("p w j -> p (w j)"),
+            )
 
         for lo, hi in WORD_GATHERS:
             nc.vector.tensor_copy(key_words[:, lo:hi], pool_words[:].bitcast(U32).indirect(listed(lo, hi)))

@@ -89,6 +89,6 @@ def tile_attend_sddmm_kernel(tc, qT, k_words, k_scales, offs, out):
         for lo, hi in SCATTERS:
             nc.vector.tensor_copy(placed[:].indirect(listed(lo, hi)), scores[:, lo:hi])
 
-        half = TOKENS // 2
-        nc.sync.dma_start(out[0, :, :half], placed[:, :half])
-        nc.scalar.dma_start(out[0, :, half:], placed[:, half:])
+        short = TOKENS // 4
+        nc.sync.dma_start(out[0, :, :short], placed[:, :short])
+        nc.scalar.dma_start(out[0, :, short:], placed[:, short:])

@@ -10,6 +10,8 @@ U16 = mybir.dt.uint16
 U8 = mybir.dt.uint8
 FP8X4 = mybir.dt.float8_e4m3fn_x4
 
+COPY = mybir.ActivationFunctionType.Copy
+
 P = 128
 PACK = 4
 SLOTS = 512
@@ -19,10 +21,10 @@ FEATURES = 512
 LIST_ROWS = 16
 FLOPS = 2 * FEATURES * QUERIES * SLOTS
 
-WORD_GATHERS = [(0, 128), (128, 256), (256, 512)]
-MATMULS = [(0, 128), (128, 256), (256, 384), (384, 512)]
+WORD_GATHERS = [(0, 128), (128, 512)]
+BANKS = [[(0, 128)], [(128, 384)], [(384, 512)]]
 EARLY_SCALES = 384
-SCATTERS = [(0, 128), (128, 512)]
+SCALAR_SLOTS = 128
 
 
 def tile_attend_sddmm_kernel(tc, qT, k_words, k_scales, offs, out):
@@ -71,23 +73,29 @@ def tile_attend_sddmm_kernel(tc, qT, k_words, k_scales, offs, out):
         for lo, hi in WORD_GATHERS:
             nc.vector.tensor_copy(key_words[:, lo:hi], pool_words[:].bitcast(U32).indirect(listed(lo, hi)))
 
-        for lo, hi in MATMULS:
-            if lo == EARLY_SCALES:
-                nc.vector.tensor_copy(key_scales[:, : hi - lo], pool_scales[:].indirect(listed(lo, hi)))
-            acc = psum.tile([P, hi - lo], F32, name="acc%d" % lo)
-            nc.tensor.matmul_mx(
-                out=acc[:],
-                lhsT=q_codes[:].bitcast(FP8X4),
-                lhsT_scale=q_scales[:],
-                rhs=key_words[:, lo:hi].bitcast(FP8X4),
-                rhs_scale=key_scales[:, lo % EARLY_SCALES : lo % EARLY_SCALES + hi - lo],
-                start=True,
-                stop=True,
-            )
-            nc.scalar.copy(out=scores[:, lo:hi], in_=acc[:])
+        for passes in BANKS:
+            first, last = passes[0][0], passes[-1][1]
+            if first == EARLY_SCALES:
+                nc.vector.tensor_copy(key_scales[:, : last - first], pool_scales[:].indirect(listed(first, last)))
+            acc = psum.tile([P, last - first], F32, name="acc%d" % first)
+            for lo, hi in passes:
+                nc.tensor.matmul_mx(
+                    out=acc[:, lo - first : hi - first],
+                    lhsT=q_codes[:].bitcast(FP8X4),
+                    lhsT_scale=q_scales[:],
+                    rhs=key_words[:, lo:hi].bitcast(FP8X4),
+                    rhs_scale=key_scales[:, lo % EARLY_SCALES : lo % EARLY_SCALES + hi - lo],
+                    start=True,
+                    stop=True,
+                )
+            if first == SCALAR_SLOTS:
+                nc.vector.tensor_copy(scores[:, first:last], acc[:])
+            else:
+                nc.scalar.copy(out=scores[:, first:last], in_=acc[:])
+            if first == 0:
+                nc.scalar.activation(placed[:].indirect(listed(0, SCALAR_SLOTS)), scores[:, :SCALAR_SLOTS], COPY)
 
-        for lo, hi in SCATTERS:
-            nc.vector.tensor_copy(placed[:].indirect(listed(lo, hi)), scores[:, lo:hi])
+        nc.vector.tensor_copy(placed[:].indirect(listed(SCALAR_SLOTS, SLOTS)), scores[:, SCALAR_SLOTS:])
 
         short = TOKENS // 4
         nc.sync.dma_start(out[0, :, :short], placed[:, :short])

@@ -48,8 +48,8 @@ def tile_attend_sddmm_kernel(tc, qT, k_words, k_scales, offs, out):
         def listed(lo, hi):
             return offsets[:, lo // LIST_ROWS : hi // LIST_ROWS]
 
-        nc.sync.dma_start(offsets[:], offs)
         nc.sync.dma_start(q_raw[:], qT[0].rearrange("(p j) w -> p j w", j=PACK))
+        nc.sync.dma_start(offsets[:], offs)
         nc.vector.memset(pool_scales[:].bitcast(I32), 0)
         for row, queue in enumerate((nc.sync, nc.scalar, nc.sync, nc.sync)):
             queue.dma_start(pool_scales[row:P:32, :].bitcast(I32), k_scales[0, row:16:4, :].bitcast(I32))
@@ -58,17 +58,15 @@ def tile_attend_sddmm_kernel(tc, qT, k_words, k_scales, offs, out):
 
         nc.vector.tensor_copy(key_scales[:], pool_scales[:].indirect(listed(0, EARLY_SCALES)))
 
-        for lo in range(0, QUERIES, QUERIES // 2):
-            hi = lo + QUERIES // 2
-            nc.scalar.copy(
-                out=q_grouped[:, lo:hi, :].rearrange("p (c i) j -> p c j i", i=4),
-                in_=q_raw[:, :, lo:hi].rearrange("p j (c i) -> p c j i", i=4),
-            )
-            nc.vector.quantize_mx(
-                out=q_codes[:, lo:hi].bitcast(FP8X4),
-                scales=q_scales[:, lo:hi],
-                in_=q_grouped[:, lo:hi, :].rearrange("p w j -> p (w j)"),
-            )
+        nc.scalar.copy(
+            out=q_grouped[:].rearrange("p (c i) j -> p c j i", i=4),
+            in_=q_raw[:].rearrange("p j (c i) -> p c j i", i=4),
+        )
+        nc.vector.quantize_mx(
+            out=q_codes[:].bitcast(FP8X4),
+            scales=q_scales[:],
+            in_=q_grouped[:].rearrange("p w j -> p (w j)"),
+        )
 
         for lo, hi in WORD_GATHERS:
             nc.vector.tensor_copy(key_words[:, lo:hi], pool_words[:].bitcast(U32).indirect(listed(lo, hi)))

@@ -21,10 +21,10 @@ FEATURES = 512
 LIST_ROWS = 16
 FLOPS = 2 * FEATURES * QUERIES * SLOTS
 
-WORD_GATHERS = [(0, 128), (128, 512)]
-BANKS = [[(0, 128)], [(128, 384)], [(384, 512)]]
+WORD_GATHERS = [(0, 128), (128, 192), (192, 512)]
+BANKS = [[(0, 128)], [(128, 192)], [(192, 320), (320, 384)], [(384, 512)]]
 EARLY_SCALES = 384
-SCALAR_SLOTS = 128
+SCALAR_SLOTS = 192
 
 
 def tile_attend_sddmm_kernel(tc, qT, k_words, k_scales, offs, out):
@@ -86,11 +86,11 @@ def tile_attend_sddmm_kernel(tc, qT, k_words, k_scales, offs, out):
                     start=True,
                     stop=True,
                 )
-            if first == SCALAR_SLOTS:
+            if first >= SCALAR_SLOTS:
                 nc.vector.tensor_copy(scores[:, first:last], acc[:])
             else:
                 nc.scalar.copy(out=scores[:, first:last], in_=acc[:])
-            if first == 0:
+            if last == SCALAR_SLOTS:
                 nc.scalar.activation(placed[:].indirect(listed(0, SCALAR_SLOTS)), scores[:, :SCALAR_SLOTS], COPY)
 
         nc.vector.tensor_copy(placed[:].indirect(listed(SCALAR_SLOTS, SLOTS)), scores[:, SCALAR_SLOTS:])

@@ -48,8 +48,8 @@ def tile_attend_sddmm_kernel(tc, qT, k_words, k_scales, offs, out):
         def listed(lo, hi):
             return offsets[:, lo // LIST_ROWS : hi // LIST_ROWS]
 
-        nc.sync.dma_start(q_raw[:], qT[0].rearrange("(p j) w -> p j w", j=PACK))
         nc.sync.dma_start(offsets[:], offs)
+        nc.sync.dma_start(q_raw[:], qT[0].rearrange("(p j) w -> p j w", j=PACK))
         nc.vector.memset(pool_scales[:].bitcast(I32), 0)
         for row, queue in enumerate((nc.sync, nc.scalar, nc.sync, nc.sync)):
             queue.dma_start(pool_scales[row:P:32, :].bitcast(I32), k_scales[0, row:16:4, :].bitcast(I32))
@@ -58,15 +58,17 @@ def tile_attend_sddmm_kernel(tc, qT, k_words, k_scales, offs, out):
 
         nc.vector.tensor_copy(key_scales[:], pool_scales[:].indirect(listed(0, EARLY_SCALES)))
 
-        nc.scalar.copy(
-            out=q_grouped[:].rearrange("p (c i) j -> p c j i", i=4),
-            in_=q_raw[:].rearrange("p j (c i) -> p c j i", i=4),
-        )
-        nc.vector.quantize_mx(
-            out=q_codes[:].bitcast(FP8X4),
-            scales=q_scales[:],
-            in_=q_grouped[:].rearrange("p w j -> p (w j)"),
-        )
+        for lo in range(0, QUERIES, QUERIES // 2):
+            hi = lo + QUERIES // 2
+            nc.scalar.copy(
+                out=q_grouped[:, lo:hi, :].rearrange("p (c i) j -> p c j i", i=4),
+                in_=q_raw[:, :, lo:hi].rearrange("p j (c i) -> p c j i", i=4),
+            )
+            nc.vector.quantize_mx(
+                out=q_codes[:, lo:hi].bitcast(FP8X4),
+                scales=q_scales[:, lo:hi],
+                in_=q_grouped[:, lo:hi, :].rearrange("p w j -> p (w j)"),
+            )
 
         for lo, hi in WORD_GATHERS:
             nc.vector.tensor_copy(key_words[:, lo:hi], pool_words[:].bitcast(U32).indirect(listed(lo, hi)))

@@ -11,6 +11,7 @@ U8 = mybir.dt.uint8
 FP8X4 = mybir.dt.float8_e4m3fn_x4
 
 COPY = mybir.ActivationFunctionType.Copy
+ADD = mybir.AluOpType.add
 
 P = 128
 PACK = 4
@@ -21,10 +22,11 @@ FEATURES = 512
 LIST_ROWS = 16
 FLOPS = 2 * FEATURES * QUERIES * SLOTS
 
-WORD_GATHERS = [(0, 128), (128, 192), (192, 512)]
-BANKS = [[(0, 128)], [(128, 192)], [(192, 320), (320, 384)], [(384, 512)]]
-EARLY_SCALES = 384
-SCALAR_SLOTS = 192
+QUARTER = SLOTS // 4
+WORD_GATHERS = [(0, 128), (128, 256), (256, 384), (384, 512)]
+EARLY_SCALES = 3 * QUARTER
+ADDS = [(0, 128), (128, 256), (256, 512), (512, 768), (768, 1024)]
+STORE_WIDTH = 128
 
 
 def tile_attend_sddmm_kernel(tc, qT, k_words, k_scales, offs, out):
@@ -43,18 +45,23 @@ def tile_attend_sddmm_kernel(tc, qT, k_words, k_scales, offs, out):
         key_words = keep.tile([P, SLOTS], U32, name="key_words", align_bytes=64)
         key_scales = keep.tile([P, EARLY_SCALES], U8, name="key_scales", align_bytes=64)
         scores = keep.tile([P, SLOTS], F32, name="scores", align_bytes=64)
-        placed = keep.tile([P, TOKENS], F32, name="placed", align_bytes=64)
+        placed_outer = keep.tile([P, TOKENS], F32, name="placed_outer", align_bytes=64)
+        placed_middle = keep.tile([P, TOKENS], F32, name="placed_middle", align_bytes=64)
+        merged = keep.tile([P, TOKENS], F32, name="merged", align_bytes=64)
 
         def listed(lo, hi):
             return offsets[:, lo // LIST_ROWS : hi // LIST_ROWS]
 
+        words = k_words[0].rearrange("p n t -> p (n t)").bitcast(I32)
         nc.sync.dma_start(offsets[:], offs)
         nc.sync.dma_start(q_raw[:], qT[0].rearrange("(p j) w -> p j w", j=PACK))
         nc.vector.memset(pool_scales[:].bitcast(I32), 0)
         for row, queue in enumerate((nc.sync, nc.scalar, nc.sync, nc.sync)):
             queue.dma_start(pool_scales[row:P:32, :].bitcast(I32), k_scales[0, row:16:4, :].bitcast(I32))
-        nc.sync.dma_start(pool_words[:], k_words[0].rearrange("p n t -> p (n t)").bitcast(I32))
-        nc.vector.memset(placed[:], 0.0)
+        nc.sync.dma_start(pool_words[:, : TOKENS // 2], words[:, : TOKENS // 2])
+        nc.sync.dma_start(pool_words[:, TOKENS // 2 :], words[:, TOKENS // 2 :])
+        nc.vector.memset(placed_outer[:], 0.0)
+        nc.vector.memset(placed_middle[:], 0.0)
 
         nc.vector.tensor_copy(key_scales[:], pool_scales[:].indirect(listed(0, EARLY_SCALES)))
 
@@ -73,30 +80,31 @@ def tile_attend_sddmm_kernel(tc, qT, k_words, k_scales, offs, out):
         for lo, hi in WORD_GATHERS:
             nc.vector.tensor_copy(key_words[:, lo:hi], pool_words[:].bitcast(U32).indirect(listed(lo, hi)))
 
-        for passes in BANKS:
-            first, last = passes[0][0], passes[-1][1]
-            if first == EARLY_SCALES:
-                nc.vector.tensor_copy(key_scales[:, : last - first], pool_scales[:].indirect(listed(first, last)))
-            acc = psum.tile([P, last - first], F32, name="acc%d" % first)
-            for lo, hi in passes:
-                nc.tensor.matmul_mx(
-                    out=acc[:, lo - first : hi - first],
-                    lhsT=q_codes[:].bitcast(FP8X4),
-                    lhsT_scale=q_scales[:],
-                    rhs=key_words[:, lo:hi].bitcast(FP8X4),
-                    rhs_scale=key_scales[:, lo % EARLY_SCALES : lo % EARLY_SCALES + hi - lo],
-                    start=True,
-                    stop=True,
-                )
-            if first >= SCALAR_SLOTS:
-                nc.vector.tensor_copy(scores[:, first:last], acc[:])
+        for lo in range(0, SLOTS, QUARTER):
+            hi = lo + QUARTER
+            if lo == EARLY_SCALES:
+                nc.vector.tensor_copy(key_scales[:, :QUARTER], pool_scales[:].indirect(listed(lo, hi)))
+            acc = psum.tile([P, QUARTER], F32, name="acc%d" % lo)
+            nc.tensor.matmul_mx(
+                out=acc[:],
+                lhsT=q_codes[:].bitcast(FP8X4),
+                lhsT_scale=q_scales[:],
+                rhs=key_words[:, lo:hi].bitcast(FP8X4),
+                rhs_scale=key_scales[:, lo % EARLY_SCALES : lo % EARLY_SCALES + QUARTER],
+                start=True,
+                stop=True,
+            )
+            if lo == EARLY_SCALES:
+                nc.vector.tensor_copy(placed_outer[:].indirect(listed(0, QUARTER)), scores[:, :QUARTER])
+                nc.vector.tensor_copy(scores[:, lo:hi], acc[:])
+                nc.vector.tensor_copy(placed_outer[:].indirect(listed(lo, hi)), scores[:, lo:hi])
             else:
-                nc.scalar.copy(out=scores[:, first:last], in_=acc[:])
-            if last == SCALAR_SLOTS:
-                nc.scalar.activation(placed[:].indirect(listed(0, SCALAR_SLOTS)), scores[:, :SCALAR_SLOTS], COPY)
+                nc.scalar.copy(out=scores[:, lo:hi], in_=acc[:])
+            if hi == EARLY_SCALES:
+                nc.scalar.activation(placed_middle[:].indirect(listed(QUARTER, hi)), scores[:, QUARTER:hi], COPY)
 
-        nc.vector.tensor_copy(placed[:].indirect(listed(SCALAR_SLOTS, SLOTS)), scores[:, SCALAR_SLOTS:])
-
-        short = TOKENS // 4
-        nc.sync.dma_start(out[0, :, :short], placed[:, :short])
-        nc.scalar.dma_start(out[0, :, short:], placed[:, short:])
+        for lo, hi in ADDS:
+            nc.vector.tensor_tensor(merged[:, lo:hi], placed_outer[:, lo:hi], placed_middle[:, lo:hi], ADD)
+            for first in range(lo, hi, STORE_WIDTH):
+                queue = (nc.sync, nc.scalar)[first // STORE_WIDTH % 2]
+                queue.dma_start(out[0, :, first : first + STORE_WIDTH], merged[:, first : first + STORE_WIDTH])

@@ -25,8 +25,7 @@ FLOPS = 2 * FEATURES * QUERIES * SLOTS
 QUARTER = SLOTS // 4
 WORD_GATHERS = [(0, 128), (128, 256), (256, 384), (384, 512)]
 EARLY_SCALES = 3 * QUARTER
-ADDS = [(0, 128), (128, 256), (256, 512), (512, 768), (768, 1024)]
-STORE_WIDTH = 128
+ADDS = [(0, 128), (128, 384), (384, 704), (704, 1024)]
 
 
 def tile_attend_sddmm_kernel(tc, qT, k_words, k_scales, offs, out):
@@ -105,6 +104,5 @@ def tile_attend_sddmm_kernel(tc, qT, k_words, k_scales, offs, out):
 
         for lo, hi in ADDS:
             nc.vector.tensor_tensor(merged[:, lo:hi], placed_outer[:, lo:hi], placed_middle[:, lo:hi], ADD)
-            for first in range(lo, hi, STORE_WIDTH):
-                queue = (nc.sync, nc.scalar)[first // STORE_WIDTH % 2]
-                queue.dma_start(out[0, :, first : first + STORE_WIDTH], merged[:, first : first + STORE_WIDTH])
+            for parity, queue in enumerate((nc.scalar, nc.sync)):
+                queue.dma_start(out[0, parity:QUERIES:2, lo:hi], merged[parity:P:2, lo:hi])

@@ -57,8 +57,8 @@ def tile_attend_sddmm_kernel(tc, qT, k_words, k_scales, offs, out):
         nc.vector.memset(pool_scales[:].bitcast(I32), 0)
         for row, queue in enumerate((nc.sync, nc.scalar, nc.sync, nc.sync)):
             queue.dma_start(pool_scales[row:P:32, :].bitcast(I32), k_scales[0, row:16:4, :].bitcast(I32))
-        nc.sync.dma_start(pool_words[:, : TOKENS // 2], words[:, : TOKENS // 2])
-        nc.sync.dma_start(pool_words[:, TOKENS // 2 :], words[:, TOKENS // 2 :])
+        for parity in range(2):
+            nc.sync.dma_start(pool_words[parity:P:2, :], words[parity:P:2, :])
         nc.vector.memset(placed_outer[:], 0.0)
         nc.vector.memset(placed_middle[:], 0.0)
 

@@ -51,14 +51,12 @@ def tile_attend_sddmm_kernel(tc, qT, k_words, k_scales, offs, out):
         def listed(lo, hi):
             return offsets[:, lo // LIST_ROWS : hi // LIST_ROWS]
 
-        words = k_words[0].rearrange("p n t -> p (n t)").bitcast(I32)
         nc.sync.dma_start(offsets[:], offs)
         nc.sync.dma_start(q_raw[:], qT[0].rearrange("(p j) w -> p j w", j=PACK))
         nc.vector.memset(pool_scales[:].bitcast(I32), 0)
         for row, queue in enumerate((nc.sync, nc.scalar, nc.sync, nc.sync)):
             queue.dma_start(pool_scales[row:P:32, :].bitcast(I32), k_scales[0, row:16:4, :].bitcast(I32))
-        for parity in range(2):
-            nc.sync.dma_start(pool_words[parity:P:2, :], words[parity:P:2, :])
+        nc.sync.dma_start(pool_words[:], k_words[0].rearrange("p n t -> p (n t)").bitcast(I32))
         nc.vector.memset(placed_outer[:], 0.0)
         nc.vector.memset(placed_middle[:], 0.0)
 

@@ -102,5 +102,8 @@ def tile_attend_sddmm_kernel(tc, qT, k_words, k_scales, offs, out):
 
         for lo, hi in ADDS:
             nc.vector.tensor_tensor(merged[:, lo:hi], placed_outer[:, lo:hi], placed_middle[:, lo:hi], ADD)
-            for parity, queue in enumerate((nc.scalar, nc.sync)):
-                queue.dma_start(out[0, parity:QUERIES:2, lo:hi], merged[parity:P:2, lo:hi])
+            if lo == 0:
+                nc.scalar.dma_start(out[0, :, lo:hi], merged[:, lo:hi])
+            else:
+                for parity, queue in enumerate((nc.scalar, nc.sync if hi == TOKENS else nc.scalar)):
+                    queue.dma_start(out[0, parity:QUERIES:2, lo:hi], merged[parity:P:2, lo:hi])

@@ -25,7 +25,7 @@ FLOPS = 2 * FEATURES * QUERIES * SLOTS
 QUARTER = SLOTS // 4
 WORD_GATHERS = [(0, 128), (128, 256), (256, 384), (384, 512)]
 EARLY_SCALES = 3 * QUARTER
-ADDS = [(0, 128), (128, 384), (384, 704), (704, 1024)]
+ADDS = [(0, 192, 1), (192, 512, 4), (512, 1024, 2)]
 
 
 def tile_attend_sddmm_kernel(tc, qT, k_words, k_scales, offs, out):
@@ -100,10 +100,8 @@ def tile_attend_sddmm_kernel(tc, qT, k_words, k_scales, offs, out):
             if hi == EARLY_SCALES:
                 nc.scalar.activation(placed_middle[:].indirect(listed(QUARTER, hi)), scores[:, QUARTER:hi], COPY)
 
-        for lo, hi in ADDS:
+        for lo, hi, shares in ADDS:
             nc.vector.tensor_tensor(merged[:, lo:hi], placed_outer[:, lo:hi], placed_middle[:, lo:hi], ADD)
-            if lo == 0:
-                nc.scalar.dma_start(out[0, :, lo:hi], merged[:, lo:hi])
-            else:
-                for parity, queue in enumerate((nc.scalar, nc.sync if hi == TOKENS else nc.scalar)):
-                    queue.dma_start(out[0, parity:QUERIES:2, lo:hi], merged[parity:P:2, lo:hi])
+            for share in range(shares):
+                queue = nc.sync if hi == TOKENS and share == shares - 1 else nc.scalar
+                queue.dma_start(out[0, share:QUERIES:shares, lo:hi], merged[share:P:shares, lo:hi])

from contextlib import ExitStack

import concourse.mybir as mybir

F32 = mybir.dt.float32
BF16 = mybir.dt.bfloat16
I32 = mybir.dt.int32
U32 = mybir.dt.uint32
U16 = mybir.dt.uint16
U8 = mybir.dt.uint8
FP8X4 = mybir.dt.float8_e4m3fn_x4

COPY = mybir.ActivationFunctionType.Copy
ADD = mybir.AluOpType.add

P = 128
PACK = 4
SLOTS = 512
TOKENS = 1024
QUERIES = 128
FEATURES = 512
LIST_ROWS = 16
FLOPS = 2 * FEATURES * QUERIES * SLOTS

QUARTER = SLOTS // 4
WORD_GATHERS = [(0, 128), (128, 256), (256, 384), (384, 512)]
EARLY_SCALES = 3 * QUARTER
ADDS = [(0, 192, 1), (192, 512, 4), (512, 1024, 2)]


def tile_attend_sddmm_kernel(tc, qT, k_words, k_scales, offs, out):
    nc = tc.nc
    with ExitStack() as ctx:
        keep = ctx.enter_context(tc.tile_pool(name="keep", bufs=1))
        psum = ctx.enter_context(tc.psum_pool(name="psum", bufs=1))

        offsets = keep.tile([P, SLOTS // LIST_ROWS], U16, name="offsets")
        pool_words = keep.tile([P, TOKENS], I32, name="pool_words", align_bytes=64)
        pool_scales = keep.tile([P, TOKENS], U8, name="pool_scales", align_bytes=64)
        q_raw = keep.tile([P, PACK, QUERIES], F32, name="q_raw", align_bytes=64)
        q_grouped = keep.tile([P, QUERIES, PACK], BF16, name="q_grouped", align_bytes=64)
        q_codes = keep.tile([P, QUERIES], U32, name="q_codes", align_bytes=64)
        q_scales = keep.tile([P, QUERIES], U8, name="q_scales", align_bytes=64)
        key_words = keep.tile([P, SLOTS], U32, name="key_words", align_bytes=64)
        key_scales = keep.tile([P, EARLY_SCALES], U8, name="key_scales", align_bytes=64)
        scores = keep.tile([P, SLOTS], F32, name="scores", align_bytes=64)
        placed_outer = keep.tile([P, TOKENS], F32, name="placed_outer", align_bytes=64)
        placed_middle = keep.tile([P, TOKENS], F32, name="placed_middle", align_bytes=64)
        merged = keep.tile([P, TOKENS], F32, name="merged", align_bytes=64)

        def listed(lo, hi):
            return offsets[:, lo // LIST_ROWS : hi // LIST_ROWS]

        nc.sync.dma_start(offsets[:], offs)
        nc.sync.dma_start(q_raw[:], qT[0].rearrange("(p j) w -> p j w", j=PACK))
        nc.vector.memset(pool_scales[:].bitcast(I32), 0)
        for row, queue in enumerate((nc.sync, nc.scalar, nc.sync, nc.sync)):
            queue.dma_start(pool_scales[row:P:32, :].bitcast(I32), k_scales[0, row:16:4, :].bitcast(I32))
        nc.sync.dma_start(pool_words[:], k_words[0].rearrange("p n t -> p (n t)").bitcast(I32))
        nc.vector.memset(placed_outer[:], 0.0)
        nc.vector.memset(placed_middle[:], 0.0)

        nc.vector.tensor_copy(key_scales[:], pool_scales[:].indirect(listed(0, EARLY_SCALES)))

        for lo in range(0, QUERIES, QUERIES // 2):
            hi = lo + QUERIES // 2
            nc.scalar.copy(
                out=q_grouped[:, lo:hi, :].rearrange("p (c i) j -> p c j i", i=4),
                in_=q_raw[:, :, lo:hi].rearrange("p j (c i) -> p c j i", i=4),
            )
            nc.vector.quantize_mx(
                out=q_codes[:, lo:hi].bitcast(FP8X4),
                scales=q_scales[:, lo:hi],
                in_=q_grouped[:, lo:hi, :].rearrange("p w j -> p (w j)"),
            )

        for lo, hi in WORD_GATHERS:
            nc.vector.tensor_copy(key_words[:, lo:hi], pool_words[:].bitcast(U32).indirect(listed(lo, hi)))

        for lo in range(0, SLOTS, QUARTER):
            hi = lo + QUARTER
            if lo == EARLY_SCALES:
                nc.vector.tensor_copy(key_scales[:, :QUARTER], pool_scales[:].indirect(listed(lo, hi)))
            acc = psum.tile([P, QUARTER], F32, name="acc%d" % lo)
            nc.tensor.matmul_mx(
                out=acc[:],
                lhsT=q_codes[:].bitcast(FP8X4),
                lhsT_scale=q_scales[:],
                rhs=key_words[:, lo:hi].bitcast(FP8X4),
                rhs_scale=key_scales[:, lo % EARLY_SCALES : lo % EARLY_SCALES + QUARTER],
                start=True,
                stop=True,
            )
            if lo == EARLY_SCALES:
                nc.vector.tensor_copy(placed_outer[:].indirect(listed(0, QUARTER)), scores[:, :QUARTER])
                nc.vector.tensor_copy(scores[:, lo:hi], acc[:])
                nc.vector.tensor_copy(placed_outer[:].indirect(listed(lo, hi)), scores[:, lo:hi])
            else:
                nc.scalar.copy(out=scores[:, lo:hi], in_=acc[:])
            if hi == EARLY_SCALES:
                nc.scalar.activation(placed_middle[:].indirect(listed(QUARTER, hi)), scores[:, QUARTER:hi], COPY)

        for lo, hi, shares in ADDS:
            nc.vector.tensor_tensor(merged[:, lo:hi], placed_outer[:, lo:hi], placed_middle[:, lo:hi], ADD)
            for share in range(shares):
                queue = nc.sync if hi == TOKENS and share == shares - 1 else nc.scalar
                queue.dma_start(out[0, share:QUERIES:shares, lo:hi], merged[share:P:shares, lo:hi])
